import numpy as np, ml_dtypes
CORES = [7,14,21,28,35,42,49,56,71,78,85,92,99,106,113,120]
N = 16
T = 256
ROUTE = [[[6,14,2],[14,0,15],[15,3,14],[14,11,1],[14,11,5],[9,14,1],[10,11,0],[14,9,2],[6,14,2],[1,2,14],[5,14,7],[13,11,14],[3,13,1],[14,6,12],[15,14,0],[0,14,11],[10,0,15],[14,8,6],[14,4,11],[8,14,1],[14,6,7],[3,14,1],[14,8,13],[14,5,0],[14,11,0],[14,2,6],[1,12,9],[14,9,1],[14,10,3],[12,6,10],[14,4,6],[14,0,12],[14,10,5],[14,5,8],[14,0,9],[14,4,1],[15,2,7],[1,8,14],[14,6,5],[14,5,10],[14,6,15],[14,13,11],[11,14,3],[14,1,7],[0,5,14],[13,0,1],[14,11,10],[14,5,2],[14,9,15],[14,6,1],[14,5,13],[14,13,1],[2,14,10],[6,14,15],[14,0,7],[14,11,10],[0,14,10],[14,6,12],[1,14,8],[9,6,14],[8,14,10],[14,3,1],[4,14,3],[14,3,15],[14,2,3],[7,11,14],[14,8,6],[12,5,6],[13,14,6],[14,15,0],[15,2,6],[14,15,10],[13,14,9],[14,0,3],[14,11,3],[14,4,6],[14,9,12],[10,6,0],[11,5,9],[14,7,11],[11,0,14],[2,12,3],[14,5,10],[14,1,0],[2,14,7],[1,11,9],[8,5,4],[12,10,14],[14,8,2],[14,9,10],[7,8,6],[14,9,1],[14,15,2],[0,14,6],[14,15,11],[3,6,14],[14,1,4],[2,8,3],[14,3,11],[9,14,2],[12,14,7],[14,8,6],[7,14,15],[7,2,14],[14,0,5],[14,15,11],[14,9,2],[4,14,8],[1,2,11],[14,8,4],[13,14,6],[14,6,12],[6,3,2],[12,14,1],[12,14,2],[14,8,11],[5,14,13],[2,14,6],[12,14,8],[1,14,9],[14,0,7],[3,10,14],[14,4,13],[7,12,3],[2,7,14],[8,14,11],[14,1,6],[14,12,13],[3,14,11],[6,14,12],[14,9,11],[10,1,14],[14,3,6],[9,12,14],[14,11,5],[14,4,13],[5,8,1],[1,2,6],[9,3,7],[13,14,12],[15,13,14],[15,14,4],[14,15,10],[1,14,7],[2,14,11],[2,8,13],[14,15,0],[14,5,0],[5,11,14],[14,9,15],[5,14,3],[14,2,15],[14,10,5],[15,6,14],[6,13,2],[4,14,6],[10,15,14],[14,15,5],[3,14,4],[14,0,8],[14,10,12],[10,14,7],[15,14,13],[6,14,5],[12,6,11],[14,2,6],[13,3,15],[7,5,10],[14,13,8],[14,1,3],[13,14,10],[8,3,0],[7,9,14],[14,3,8],[14,4,12],[1,2,12],[14,13,9],[1,11,14],[11,14,4],[8,14,11],[14,6,10],[13,10,14],[14,13,6],[14,12,7],[14,10,4],[5,6,14],[14,13,5],[4,14,2],[2,12,14],[3,14,0],[8,11,14],[13,0,2],[2,14,15],[14,3,13],[14,7,4],[14,8,13],[14,4,7],[12,14,7],[7,14,1],[3,12,14],[15,11,8],[10,3,14],[6,7,9],[14,13,6],[10,11,2],[14,11,9],[2,7,3],[3,1,15],[14,1,7],[12,4,14],[14,5,6],[14,4,0],[7,14,12],[14,2,5],[2,14,5],[4,14,9],[12,2,1],[4,14,6],[2,4,14],[7,3,8],[1,4,14],[14,7,10],[1,14,12],[14,6,12],[14,5,4],[14,11,3],[12,14,0],[9,3,12],[14,12,2],[8,14,4],[7,6,14],[6,9,14],[5,1,14],[14,15,3],[2,12,15],[11,0,14],[14,3,2],[14,15,0],[14,0,13],[6,14,0],[14,13,2],[9,12,4],[1,4,14],[14,7,6],[12,10,14],[4,14,1],[14,15,12],[14,10,2],[15,14,4],[14,2,8],[14,2,3],[7,14,10],[14,12,9],[14,6,9],[14,3,13],[14,4,8]],[[1,14,2],[4,5,8],[1,14,5],[14,4,8],[14,11,8],[8,6,14],[5,10,3],[0,6,11],[7,14,11],[14,15,2],[15,14,7],[8,2,9],[2,6,14],[14,0,12],[1,14,9],[14,10,12],[14,3,10],[9,1,8],[14,6,10],[15,6,4],[2,14,0],[0,7,4],[14,11,10],[8,14,2],[1,14,0],[1,5,14],[14,4,11],[14,15,13],[9,14,11],[14,7,11],[6,9,7],[11,15,6],[14,2,7],[6,12,14],[10,14,9],[15,12,9],[14,11,10],[14,12,6],[0,11,1],[5,14,9],[14,8,13],[12,14,6],[1,6,14],[8,14,7],[3,14,9],[14,8,9],[13,3,11],[0,14,4],[14,0,12],[0,6,9],[1,9,14],[14,8,4],[15,11,8],[9,4,12],[13,14,5],[6,14,7],[12,9,14],[14,11,4],[10,14,4],[0,6,14],[14,8,1],[14,15,2],[6,5,2],[14,8,7],[9,14,10],[9,3,14],[14,15,4],[2,11,14],[14,2,8],[3,14,4],[14,7,4],[7,5,4],[5,7,13],[4,3,14],[8,6,5],[14,1,8],[4,14,12],[10,0,7],[8,15,3],[13,12,11],[14,3,7],[14,11,9],[14,0,7],[14,10,11],[4,5,1],[14,12,2],[0,8,14],[9,12,14],[15,14,6],[14,12,5],[6,2,0],[15,2,14],[14,2,5],[15,12,0],[8,9,14],[10,2,13],[14,10,4],[9,14,2],[15,14,8],[4,7,14],[14,15,12],[4,8,13],[10,7,4],[10,1,6],[10,5,8],[14,7,1],[12,6,0],[14,9,15],[14,12,13],[13,4,7],[11,15,0],[9,14,1],[5,14,2],[11,14,6],[4,10,5],[11,14,3],[14,6,13],[1,11,3],[5,14,8],[9,14,6],[14,2,6],[14,8,10],[1,9,4],[15,9,10],[10,3,1],[6,15,11],[10,1,14],[14,6,1],[13,12,6],[12,11,14],[14,4,12],[13,1,14],[15,1,0],[10,9,14],[14,15,8],[14,8,12],[14,10,4],[14,10,9],[14,0,15],[14,1,7],[13,15,8],[1,14,7],[5,14,2],[10,14,5],[3,4,14],[14,1,12],[2,8,14],[13,9,14],[14,0,15],[14,0,13],[14,12,13],[14,10,12],[11,14,5],[14,1,4],[4,14,7],[4,14,11],[14,4,1],[13,8,14],[1,14,7],[0,14,1],[14,15,1],[12,13,0],[14,15,6],[14,7,15],[14,1,8],[1,10,11],[3,14,4],[8,6,7],[14,3,0],[14,15,3],[14,1,3],[3,8,14],[9,6,14],[15,14,13],[8,14,12],[1,14,9],[10,12,14],[5,14,8],[1,10,2],[12,14,6],[14,12,9],[1,11,8],[9,3,14],[14,12,2],[5,14,10],[10,14,5],[14,4,10],[2,14,12],[14,4,13],[14,13,7],[11,2,14],[14,15,9],[13,14,12],[14,3,0],[10,14,6],[14,10,0],[11,5,14],[14,1,12],[1,14,9],[14,2,0],[14,11,1],[14,0,11],[14,4,12],[14,15,4],[4,3,14],[14,12,5],[14,15,7],[8,14,5],[15,11,2],[14,11,2],[14,15,0],[5,1,6],[13,14,9],[8,10,14],[14,6,10],[14,11,5],[14,11,4],[3,14,5],[14,1,0],[14,8,10],[14,2,0],[14,13,0],[1,14,15],[14,3,5],[1,15,3],[15,8,14],[14,8,6],[15,14,5],[14,12,8],[14,2,10],[1,4,14],[9,12,5],[0,14,6],[14,13,1],[14,8,7],[13,14,9],[4,3,14],[14,6,11],[13,8,14],[14,9,8],[5,14,9],[9,12,14],[4,14,12],[14,4,1],[4,6,14],[14,3,9],[14,8,11],[4,5,13],[14,1,15],[14,15,0],[3,14,15],[13,0,14],[0,8,12],[14,2,5],[14,4,3],[15,14,5]],[[14,5,1],[5,14,4],[2,14,4],[9,14,15],[12,7,14],[14,5,2],[4,14,15],[14,11,0],[8,10,9],[14,11,13],[3,10,14],[11,7,6],[1,14,15],[14,11,13],[15,3,9],[14,8,11],[4,14,2],[12,3,1],[14,5,8],[14,9,13],[11,14,13],[14,5,11],[14,4,13],[0,9,1],[5,4,14],[6,5,7],[7,4,5],[14,9,11],[9,14,11],[14,11,15],[13,11,8],[0,14,1],[14,0,9],[14,7,0],[3,14,4],[2,14,12],[9,7,14],[14,12,2],[1,15,14],[14,10,8],[14,6,11],[14,3,0],[14,2,6],[14,15,3],[15,7,14],[9,5,2],[14,5,3],[4,0,14],[14,12,0],[5,0,14],[14,12,8],[14,3,12],[1,14,3],[0,14,12],[7,11,12],[4,14,3],[2,0,3],[14,5,15],[6,14,1],[14,4,11],[15,13,14],[14,4,11],[15,5,14],[14,0,13],[14,3,12],[14,9,3],[9,0,3],[14,13,8],[5,14,10],[0,12,4],[11,6,13],[14,12,6],[6,11,0],[13,14,7],[15,1,5],[9,15,11],[9,14,11],[14,13,5],[10,1,11],[2,14,15],[14,4,2],[14,1,6],[1,14,5],[2,10,14],[12,14,2],[6,15,1],[14,1,9],[14,9,8],[10,11,14],[15,1,14],[14,3,4],[1,2,14],[5,14,6],[2,14,6],[10,9,5],[15,8,14],[14,12,9],[6,4,14],[4,2,11],[2,14,9],[5,10,4],[14,9,4],[1,14,12],[14,10,4],[4,6,10],[8,7,12],[12,14,3],[14,11,9],[3,2,12],[14,10,13],[9,11,1],[14,11,9],[15,2,1],[1,2,14],[14,3,13],[0,14,10],[7,14,9],[14,7,2],[10,11,14],[10,3,1],[6,1,7],[12,14,8],[2,4,8],[3,14,8],[5,14,12],[5,14,7],[8,14,6],[14,3,4],[14,8,9],[0,15,14],[14,0,4],[14,15,12],[9,12,14],[14,8,15],[10,7,14],[4,5,14],[6,14,13],[7,14,4],[1,14,15],[14,13,10],[14,13,3],[2,14,12],[8,4,11],[5,7,14],[10,4,13],[10,5,14],[14,7,12],[7,1,9],[14,6,1],[8,14,10],[14,1,12],[14,15,11],[14,7,11],[3,15,14],[12,14,11],[10,9,14],[11,14,9],[9,14,10],[14,6,4],[14,9,3],[2,14,6],[14,2,10],[14,8,3],[14,11,2],[13,12,14],[6,13,9],[14,4,3],[14,15,7],[1,0,3],[1,13,14],[11,6,14],[1,7,6],[9,1,14],[14,9,3],[14,8,4],[14,2,13],[14,0,9],[1,0,14],[7,10,14],[14,6,3],[14,11,6],[10,2,1],[12,9,14],[9,14,5],[14,5,15],[14,8,11],[14,15,8],[4,13,0],[0,2,14],[1,11,14],[14,3,15],[5,14,6],[14,4,13],[14,9,1],[0,3,6],[15,14,7],[14,4,10],[14,9,0],[13,9,14],[0,9,14],[9,0,14],[6,0,14],[14,13,4],[13,3,14],[14,13,0],[14,12,5],[4,14,11],[14,11,6],[6,14,0],[6,11,5],[15,3,11],[14,15,10],[9,14,12],[4,11,3],[14,9,4],[0,14,4],[14,15,3],[13,14,8],[7,15,8],[14,5,8],[14,8,9],[14,9,13],[14,9,3],[1,13,14],[14,3,6],[7,14,8],[14,10,3],[14,8,2],[13,4,3],[4,14,15],[9,14,1],[14,3,8],[14,4,7],[1,14,12],[8,14,1],[1,14,3],[0,14,4],[14,9,0],[1,14,0],[6,14,13],[14,4,1],[14,1,13],[14,9,8],[2,15,14],[8,1,14],[14,5,2],[6,14,5],[14,15,1],[14,10,1],[14,9,11],[14,13,10],[14,3,12],[4,14,9],[0,14,3],[5,14,11],[0,9,14]],[[5,14,7],[9,10,1],[6,14,11],[14,9,4],[14,0,4],[6,5,11],[9,11,8],[10,14,15],[14,8,6],[1,0,4],[10,14,8],[14,0,9],[11,1,0],[5,11,14],[2,8,14],[0,14,9],[7,0,10],[14,12,8],[14,12,3],[3,12,14],[7,1,14],[14,4,8],[14,0,9],[14,13,10],[7,14,8],[2,11,14],[14,11,9],[14,9,4],[14,13,4],[4,5,14],[14,11,13],[14,1,12],[12,1,11],[8,10,0],[14,11,2],[7,11,12],[13,14,11],[12,2,14],[14,8,13],[14,11,9],[8,4,9],[14,1,7],[14,13,12],[15,0,14],[14,13,10],[14,0,6],[14,2,1],[11,13,9],[14,13,4],[4,14,5],[14,8,10],[2,10,8],[14,10,7],[14,9,5],[1,14,7],[1,14,7],[6,5,10],[14,6,5],[2,14,5],[11,14,13],[14,1,5],[14,6,7],[14,4,12],[4,14,7],[14,8,15],[12,14,4],[13,3,7],[12,13,8],[10,14,13],[14,5,4],[1,11,5],[14,8,0],[5,14,1],[8,12,14],[3,14,7],[9,14,7],[4,1,14],[4,0,14],[14,7,12],[14,7,6],[3,11,2],[6,10,14],[14,4,7],[6,14,10],[0,15,14],[14,10,12],[8,14,15],[3,14,2],[4,14,10],[7,14,11],[9,14,8],[14,12,5],[14,6,0],[10,14,0],[14,13,0],[14,15,3],[1,9,3],[7,14,9],[7,11,15],[7,1,3],[14,1,10],[1,14,9],[7,0,2],[15,14,6],[14,12,2],[7,15,14],[6,9,14],[7,10,14],[4,5,14],[14,4,8],[14,8,9],[0,14,7],[14,8,7],[14,15,11],[4,15,14],[14,15,2],[4,14,3],[5,7,10],[14,0,15],[14,9,7],[14,15,9],[14,4,7],[14,0,10],[14,12,11],[14,5,11],[14,6,9],[7,10,1],[5,14,11],[14,4,12],[14,9,12],[14,7,2],[5,14,10],[14,6,12],[11,14,2],[14,12,3],[14,0,6],[14,3,0],[4,15,12],[14,6,12],[14,3,12],[14,11,9],[1,2,14],[8,14,4],[2,0,14],[14,4,3],[2,14,12],[14,1,12],[3,6,14],[14,12,3],[12,15,14],[8,11,14],[7,0,14],[4,1,7],[3,7,8],[9,4,13],[1,14,12],[14,12,7],[6,9,10],[13,8,0],[1,4,14],[14,11,7],[15,6,3],[14,0,3],[10,14,2],[4,14,6],[14,11,15],[2,14,12],[14,7,0],[13,2,15],[14,9,15],[4,3,5],[14,8,13],[11,14,6],[8,14,15],[14,4,11],[15,6,14],[2,14,13],[14,10,2],[7,13,4],[14,5,13],[3,4,9],[14,11,1],[12,14,11],[6,14,4],[1,14,2],[6,14,9],[0,7,14],[1,14,9],[14,5,4],[10,14,0],[14,3,5],[15,11,14],[5,12,1],[14,8,15],[3,5,14],[14,0,6],[5,2,14],[9,14,2],[9,3,12],[14,0,12],[3,11,14],[12,8,0],[14,7,4],[11,14,15],[14,7,6],[15,9,14],[8,11,14],[12,13,14],[11,1,8],[14,5,2],[3,14,15],[6,2,12],[2,13,14],[14,10,9],[2,14,11],[4,10,6],[14,0,11],[8,14,7],[14,0,15],[8,15,14],[14,9,11],[0,2,14],[14,7,13],[7,11,10],[10,14,12],[14,8,10],[11,14,0],[14,3,12],[14,11,15],[13,14,5],[14,8,3],[15,12,3],[1,0,10],[14,8,0],[14,0,11],[10,5,14],[6,13,14],[14,8,6],[9,15,14],[14,6,13],[14,10,9],[7,9,6],[14,7,5],[9,14,3],[2,14,12],[1,6,0],[14,10,12],[14,1,4],[9,13,6],[4,14,11],[9,8,14],[14,4,10],[6,14,7],[14,0,1],[14,13,12],[14,5,2]],[[15,2,0],[0,12,14],[6,0,14],[4,8,14],[14,7,9],[15,7,6],[14,6,2],[0,14,10],[14,13,0],[14,7,0],[14,11,3],[15,14,11],[14,3,1],[8,11,1],[7,11,14],[14,1,13],[8,5,6],[9,12,10],[14,12,7],[14,1,8],[9,2,14],[9,14,0],[0,10,14],[14,5,4],[0,1,14],[12,2,7],[0,11,14],[7,0,14],[14,12,6],[13,7,14],[2,14,12],[12,15,10],[11,14,12],[14,0,4],[10,1,4],[4,5,14],[14,15,2],[1,7,14],[14,5,13],[14,6,3],[14,13,4],[3,12,6],[9,0,14],[11,14,5],[14,1,3],[15,14,4],[0,7,13],[11,14,10],[14,5,0],[14,10,8],[15,14,3],[9,0,2],[10,14,4],[3,14,10],[5,4,13],[14,10,11],[11,10,6],[5,6,11],[7,14,1],[12,14,10],[6,12,2],[14,1,11],[12,14,7],[1,14,2],[14,13,6],[14,1,11],[14,12,11],[14,9,10],[7,0,14],[6,15,3],[14,4,12],[1,12,5],[15,3,7],[8,7,0],[14,0,9],[14,2,11],[6,14,0],[2,11,7],[14,0,11],[14,8,0],[7,14,0],[14,9,10],[5,15,1],[0,14,6],[6,14,5],[15,2,12],[14,10,9],[13,2,14],[3,14,11],[14,11,10],[10,14,3],[3,9,14],[4,14,2],[13,4,1],[0,10,14],[14,4,3],[14,10,9],[3,11,14],[3,7,14],[0,9,6],[13,7,1],[14,9,0],[14,4,1],[9,15,5],[14,5,7],[15,11,5],[14,1,13],[10,14,11],[14,3,8],[14,7,8],[10,5,1],[2,8,14],[14,4,2],[11,14,6],[1,14,13],[14,6,13],[6,14,11],[7,12,15],[13,14,7],[10,4,8],[14,2,8],[14,15,13],[12,14,2],[3,7,6],[11,15,14],[5,14,9],[11,14,1],[5,6,9],[9,14,11],[14,3,0],[8,12,14],[14,4,0],[4,7,14],[14,1,7],[14,9,4],[14,5,9],[10,14,6],[14,7,2],[14,13,15],[14,9,1],[5,14,7],[0,14,5],[15,6,5],[14,12,8],[6,14,13],[11,9,14],[14,2,7],[14,6,13],[12,14,7],[9,14,12],[14,10,2],[6,9,14],[4,3,11],[14,7,10],[1,9,15],[0,14,4],[2,14,11],[14,11,15],[14,10,7],[7,14,3],[8,4,14],[12,14,1],[14,7,6],[11,4,2],[5,2,14],[14,0,15],[14,3,4],[14,10,5],[14,4,11],[4,5,11],[14,6,7],[6,9,7],[14,7,9],[0,7,4],[9,4,15],[14,9,10],[14,0,8],[3,14,2],[15,12,14],[14,3,5],[4,0,2],[14,12,15],[14,12,5],[12,14,10],[14,10,7],[1,14,11],[14,8,11],[14,10,3],[14,5,13],[14,4,8],[5,3,7],[14,12,2],[15,14,1],[14,12,1],[14,13,11],[14,12,8],[9,14,6],[7,14,13],[14,10,7],[14,4,6],[14,11,2],[9,1,14],[14,3,0],[14,10,12],[14,12,3],[2,9,14],[3,14,1],[0,8,11],[10,14,9],[15,0,11],[2,14,3],[8,14,13],[11,14,6],[6,12,7],[10,11,12],[11,4,1],[14,13,11],[3,14,6],[15,3,14],[2,3,14],[10,8,14],[14,11,15],[13,14,3],[13,14,4],[10,14,15],[0,1,14],[14,0,1],[14,12,4],[0,1,2],[14,7,0],[14,9,11],[14,8,13],[14,6,8],[2,14,6],[3,4,14],[14,10,6],[14,0,8],[14,3,11],[8,4,2],[14,4,3],[3,15,13],[6,14,1],[14,9,8],[10,14,3],[14,5,11],[3,14,6],[8,7,14],[11,14,0],[14,4,8],[14,6,10],[2,8,14],[0,13,6],[14,12,5],[14,6,2],[10,15,1],[14,9,10]],[[14,0,7],[12,6,7],[13,14,15],[14,1,5],[14,6,10],[3,9,2],[0,4,14],[14,13,9],[6,14,5],[10,11,8],[7,14,3],[11,9,15],[14,9,10],[11,12,0],[14,1,10],[14,11,0],[9,14,12],[14,12,10],[7,14,2],[6,2,15],[9,14,11],[14,8,13],[9,2,7],[4,14,2],[11,2,6],[0,1,15],[14,15,1],[15,14,0],[4,12,14],[14,10,7],[11,13,14],[14,8,11],[14,13,5],[7,14,12],[3,10,14],[12,0,14],[14,11,13],[3,12,14],[8,14,7],[6,15,14],[14,3,8],[14,4,3],[14,13,7],[14,9,7],[13,10,7],[7,11,5],[14,7,6],[3,7,1],[4,5,9],[8,4,7],[14,6,13],[1,14,0],[7,12,0],[4,14,0],[5,14,3],[14,1,8],[9,14,10],[7,5,4],[13,14,11],[14,3,9],[5,7,14],[14,8,15],[14,4,2],[14,15,3],[14,8,13],[13,11,14],[14,6,13],[14,1,10],[8,14,7],[14,2,4],[14,7,6],[14,9,7],[7,14,8],[11,14,15],[5,2,6],[14,2,3],[14,6,0],[14,3,12],[15,4,14],[14,7,11],[15,14,3],[6,15,8],[14,10,13],[14,9,3],[0,6,2],[14,9,6],[6,14,0],[14,9,7],[13,14,0],[14,13,8],[14,5,9],[8,5,0],[8,9,12],[4,0,14],[14,8,11],[14,11,15],[6,14,5],[14,4,9],[11,14,9],[14,8,13],[8,15,13],[11,14,9],[14,10,13],[15,14,3],[14,13,5],[14,5,11],[14,6,15],[15,14,3],[3,15,4],[12,15,14],[4,14,10],[4,13,14],[6,13,14],[7,0,14],[12,2,14],[15,12,7],[9,14,2],[4,7,1],[14,5,1],[5,4,7],[6,2,14],[14,11,7],[14,2,7],[14,2,13],[3,8,2],[13,14,0],[13,3,2],[14,11,7],[14,5,3],[14,9,11],[1,5,10],[14,11,8],[4,14,0],[14,4,11],[12,9,3],[0,14,10],[8,12,4],[14,3,7],[13,0,1],[1,14,9],[14,7,9],[8,15,3],[8,6,14],[12,1,14],[14,7,8],[12,1,7],[0,14,6],[14,5,3],[14,12,11],[13,3,15],[14,8,7],[1,14,9],[14,11,7],[11,14,4],[11,14,3],[14,0,13],[15,14,12],[14,2,10],[0,9,14],[11,14,0],[3,11,14],[10,7,2],[0,14,3],[14,10,1],[14,10,15],[13,7,14],[2,8,12],[14,15,5],[14,8,0],[2,0,10],[0,8,14],[14,12,0],[6,15,14],[11,6,2],[14,9,12],[10,9,11],[14,5,10],[14,8,9],[12,3,14],[13,14,4],[3,14,13],[14,12,5],[8,2,7],[14,1,11],[14,13,5],[14,15,4],[11,7,14],[10,4,3],[14,1,11],[14,8,0],[14,8,10],[5,3,14],[14,12,11],[2,12,14],[14,9,2],[14,0,2],[14,2,12],[14,3,7],[0,6,8],[14,13,8],[14,11,12],[14,8,12],[11,1,7],[14,0,1],[0,13,14],[14,9,0],[11,0,9],[14,15,6],[14,4,9],[14,13,1],[11,14,2],[6,14,7],[14,7,1],[15,14,7],[0,10,14],[14,5,3],[14,6,9],[14,10,6],[14,0,5],[14,9,0],[15,14,7],[2,14,10],[14,7,4],[14,0,13],[8,11,14],[3,6,14],[7,15,14],[14,3,4],[10,14,3],[1,13,0],[9,1,14],[14,1,10],[14,7,6],[9,12,2],[5,12,14],[14,10,13],[10,11,14],[6,9,14],[3,5,14],[14,8,11],[14,3,7],[14,1,6],[12,14,13],[14,1,3],[9,14,11],[14,5,12],[14,6,10],[14,8,15],[15,14,13],[7,5,1],[7,14,5],[3,14,7],[13,4,15],[1,14,6],[14,12,6],[5,13,1]],[[14,9,13],[14,10,6],[14,1,11],[14,1,4],[8,14,15],[5,1,12],[14,11,4],[14,1,13],[13,10,6],[14,10,9],[14,10,4],[14,6,8],[14,6,15],[14,7,15],[11,3,4],[14,3,6],[5,14,7],[14,2,10],[12,14,4],[4,14,11],[14,15,9],[14,11,1],[11,4,5],[14,1,4],[14,10,13],[1,12,9],[15,14,0],[11,14,1],[15,14,3],[10,1,4],[0,7,13],[14,0,13],[4,3,12],[7,0,13],[0,8,14],[14,13,7],[10,11,14],[0,14,11],[15,1,9],[3,14,13],[5,4,12],[14,10,13],[14,15,6],[14,13,6],[4,14,10],[9,15,4],[14,4,7],[12,14,10],[11,14,10],[14,4,1],[13,15,14],[14,5,10],[12,13,14],[3,15,14],[0,10,14],[14,13,15],[13,14,2],[14,2,8],[11,2,14],[2,14,11],[14,12,8],[14,12,8],[14,10,7],[14,15,7],[14,15,7],[14,3,11],[0,14,11],[14,12,4],[6,14,2],[15,14,10],[14,13,9],[2,10,11],[8,14,7],[5,14,6],[14,11,12],[12,11,14],[14,4,6],[6,2,12],[7,14,6],[11,10,4],[14,13,2],[15,2,1],[2,11,14],[7,9,11],[3,14,0],[14,13,15],[14,3,8],[14,1,3],[14,3,13],[11,15,6],[10,12,5],[6,11,4],[3,5,14],[0,14,8],[0,4,14],[14,9,12],[12,15,11],[14,6,12],[10,5,14],[0,14,1],[14,1,10],[12,6,7],[14,5,2],[14,11,13],[15,3,14],[14,15,3],[6,2,14],[14,8,6],[14,1,15],[14,1,11],[2,14,9],[15,9,3],[8,14,6],[14,11,12],[14,12,8],[14,10,8],[14,0,15],[7,11,8],[14,7,4],[8,9,14],[15,9,11],[14,7,8],[13,1,15],[6,5,9],[15,11,14],[14,1,6],[5,13,14],[2,10,14],[11,7,5],[14,10,2],[3,14,6],[13,6,11],[14,15,7],[9,4,7],[13,10,14],[14,15,1],[14,6,8],[14,4,15],[14,5,6],[14,8,7],[0,14,7],[10,14,3],[14,13,9],[10,2,5],[14,10,15],[14,6,10],[4,6,14],[14,2,0],[12,14,3],[4,11,1],[8,14,1],[7,14,5],[7,14,8],[14,13,1],[8,9,14],[14,6,13],[1,0,14],[12,10,4],[14,5,3],[14,9,11],[11,0,15],[14,8,11],[8,7,10],[14,5,2],[14,13,7],[4,0,14],[14,3,1],[2,14,1],[4,14,7],[14,2,8],[14,10,4],[14,13,0],[7,14,2],[14,7,11],[5,4,14],[14,5,9],[14,9,4],[14,12,5],[14,11,2],[14,0,10],[8,14,2],[14,7,10],[4,3,10],[13,14,12],[15,0,11],[14,11,13],[3,14,6],[15,6,1],[11,7,5],[6,14,11],[11,5,14],[1,14,12],[14,12,7],[1,8,3],[14,5,15],[14,10,3],[14,13,4],[5,14,13],[14,9,0],[1,14,6],[3,14,6],[12,13,14],[11,14,8],[8,9,4],[7,0,5],[2,14,9],[9,8,1],[14,9,15],[14,9,7],[9,15,6],[14,15,7],[14,9,12],[14,3,9],[2,7,14],[14,7,8],[14,12,3],[14,8,3],[12,14,15],[14,13,0],[14,0,5],[14,2,10],[0,10,1],[15,14,0],[0,14,13],[14,6,2],[13,9,12],[0,3,8],[11,2,0],[14,8,10],[14,9,8],[14,4,7],[7,14,2],[6,14,10],[4,14,6],[12,2,8],[11,14,10],[14,11,4],[8,9,10],[14,12,7],[14,5,8],[2,10,15],[8,14,7],[11,14,10],[0,14,8],[14,1,9],[15,14,6],[3,14,10],[14,7,9],[14,9,5],[14,8,10],[13,1,15],[4,14,0],[14,11,8],[12,8,14],[14,2,8],[14,7,12]],[[10,14,15],[14,11,7],[14,5,12],[7,2,4],[12,4,14],[6,10,14],[14,12,8],[14,5,12],[14,6,10],[13,2,14],[10,14,12],[8,1,11],[10,7,9],[2,5,8],[2,14,10],[5,14,9],[12,11,9],[14,15,9],[11,14,0],[9,8,5],[14,4,8],[12,14,9],[5,6,13],[14,13,5],[14,5,8],[14,8,0],[7,3,14],[1,2,14],[13,7,14],[14,1,3],[15,14,1],[12,14,4],[8,9,11],[0,14,3],[9,14,0],[14,5,7],[14,7,9],[15,14,6],[2,14,0],[14,12,9],[13,0,6],[10,14,12],[1,0,14],[8,14,9],[10,0,14],[14,0,15],[14,15,11],[6,0,14],[14,9,12],[9,3,1],[13,12,14],[3,14,5],[14,15,2],[13,14,5],[8,2,6],[2,4,14],[2,14,5],[7,14,13],[14,13,15],[14,2,11],[7,13,1],[14,4,7],[0,14,3],[14,15,3],[14,1,11],[14,12,2],[14,2,6],[14,1,11],[2,3,14],[14,0,9],[14,0,3],[12,14,9],[14,8,2],[11,0,14],[3,14,2],[14,5,9],[12,11,2],[14,15,2],[14,9,1],[14,12,7],[14,8,5],[6,14,3],[14,12,3],[14,6,4],[10,11,9],[2,14,12],[14,13,5],[1,14,13],[14,3,15],[10,9,14],[12,14,3],[0,11,5],[14,10,8],[12,14,11],[5,15,14],[7,14,12],[12,11,8],[1,14,6],[14,2,15],[14,1,10],[6,14,11],[8,9,0],[1,9,14],[14,1,13],[11,12,8],[13,14,0],[14,1,2],[4,11,14],[15,3,5],[11,14,15],[11,7,13],[10,3,14],[14,10,4],[14,7,8],[0,15,4],[9,10,14],[2,14,6],[14,11,9],[14,5,1],[3,6,8],[14,6,5],[14,10,12],[4,15,3],[14,9,12],[6,15,7],[8,0,3],[10,5,14],[5,14,3],[14,13,3],[14,12,9],[13,7,2],[14,9,1],[14,1,11],[14,1,12],[14,7,0],[3,14,0],[5,0,9],[10,14,8],[1,14,8],[10,9,11],[14,2,13],[9,14,5],[2,14,6],[1,14,10],[12,1,14],[6,0,14],[14,15,10],[14,3,12],[9,14,7],[14,15,8],[14,4,7],[0,14,8],[10,14,11],[14,0,2],[14,1,5],[14,2,12],[1,12,0],[14,0,10],[8,14,12],[7,14,8],[13,1,8],[6,14,3],[13,11,6],[15,14,2],[4,0,8],[14,6,13],[1,13,4],[14,3,12],[3,14,1],[14,1,12],[14,12,10],[14,9,4],[12,14,8],[3,14,4],[14,13,8],[10,14,15],[14,11,5],[14,15,10],[14,5,0],[15,6,14],[11,3,15],[14,0,9],[14,3,8],[1,13,11],[4,14,3],[14,8,11],[14,13,1],[13,2,14],[12,11,8],[14,2,4],[14,2,15],[14,0,2],[14,3,4],[14,15,10],[10,14,1],[6,12,14],[14,6,0],[14,3,0],[10,14,11],[14,10,3],[14,2,15],[12,14,15],[14,6,1],[13,14,3],[15,14,5],[12,4,14],[14,11,6],[5,14,3],[8,14,15],[10,15,0],[0,12,14],[14,2,7],[14,3,1],[6,14,12],[14,11,6],[14,12,3],[6,14,4],[3,14,15],[8,14,1],[14,3,6],[2,14,12],[14,6,9],[13,10,15],[15,5,1],[4,2,14],[14,3,4],[14,2,13],[14,2,11],[14,12,1],[2,11,4],[2,14,8],[14,9,2],[14,10,1],[14,10,2],[14,9,0],[13,14,1],[11,14,15],[0,4,14],[13,14,0],[14,10,4],[14,1,13],[10,14,12],[5,14,12],[1,0,8],[2,14,13],[1,0,14],[5,4,7],[3,14,13],[1,14,13],[14,13,4],[14,13,12],[14,5,13],[14,6,8],[0,4,8],[15,13,14],[14,13,4]],[[3,14,2],[5,2,1],[1,0,14],[13,14,11],[14,15,4],[1,2,10],[2,14,10],[8,0,5],[11,14,12],[15,10,3],[11,9,10],[0,14,10],[12,8,11],[7,14,10],[14,6,10],[14,12,9],[10,14,4],[14,15,8],[13,14,0],[14,7,8],[15,14,8],[14,6,4],[1,14,10],[14,4,0],[13,5,14],[11,0,14],[1,10,6],[14,4,15],[14,1,10],[11,14,2],[6,10,0],[14,9,12],[2,8,5],[14,8,5],[14,6,11],[8,14,1],[14,8,15],[14,12,4],[2,14,4],[2,14,3],[3,1,4],[14,10,9],[15,11,12],[14,0,2],[14,15,8],[10,7,1],[14,8,1],[12,14,2],[9,14,2],[14,1,4],[14,9,12],[14,6,0],[14,1,8],[14,8,9],[14,10,12],[14,1,15],[6,14,11],[2,14,4],[2,4,12],[14,12,7],[4,7,14],[14,10,3],[3,14,7],[1,14,15],[14,9,15],[8,0,1],[12,14,6],[14,12,1],[14,2,10],[7,14,1],[14,5,6],[0,8,14],[14,6,3],[10,15,14],[14,5,3],[12,14,6],[15,14,6],[14,9,0],[4,3,12],[7,14,3],[1,10,14],[14,3,0],[14,11,12],[15,14,12],[14,1,11],[0,14,2],[14,8,4],[14,11,12],[14,15,2],[0,14,5],[0,4,14],[13,0,9],[14,5,7],[9,8,1],[14,8,9],[13,14,2],[14,3,15],[2,14,0],[4,14,3],[11,2,12],[2,8,14],[11,13,8],[11,15,10],[14,7,15],[14,7,6],[3,14,11],[14,3,12],[10,14,15],[12,6,14],[2,10,0],[3,14,12],[14,15,12],[14,0,1],[13,14,0],[11,15,0],[3,14,7],[1,9,10],[4,14,6],[15,14,6],[14,10,8],[14,3,6],[13,14,11],[8,15,14],[2,7,14],[14,9,6],[3,7,14],[14,12,8],[14,11,13],[14,6,7],[14,2,11],[6,14,10],[6,5,15],[14,8,12],[15,7,14],[6,14,2],[13,8,14],[14,6,13],[7,1,14],[14,4,15],[9,15,12],[13,2,5],[1,8,4],[1,14,7],[14,1,7],[3,9,15],[3,14,13],[14,13,9],[1,15,0],[14,15,9],[15,9,6],[10,14,4],[1,13,14],[14,10,15],[14,8,0],[11,10,2],[9,14,3],[15,5,14],[5,14,0],[6,10,4],[6,10,14],[2,7,14],[1,13,14],[14,5,8],[0,14,4],[14,15,4],[0,4,14],[14,13,12],[10,15,9],[14,8,9],[14,13,3],[4,5,14],[10,12,14],[14,8,0],[14,1,6],[1,0,15],[5,0,14],[14,9,1],[14,13,2],[14,5,11],[14,15,4],[14,7,15],[10,2,14],[14,9,12],[14,11,10],[5,14,12],[14,13,0],[4,14,13],[3,14,13],[14,4,3],[6,14,12],[4,14,3],[14,8,10],[5,1,4],[7,13,14],[14,9,12],[7,15,11],[1,14,15],[14,7,1],[13,14,1],[1,3,14],[8,14,5],[14,11,15],[0,14,10],[6,14,11],[12,3,13],[11,14,2],[14,0,3],[8,2,14],[8,3,14],[10,0,14],[14,13,5],[15,14,4],[10,14,5],[15,3,11],[9,4,14],[15,11,14],[5,13,6],[14,9,10],[14,5,12],[14,8,13],[14,13,12],[4,7,13],[6,1,14],[14,10,12],[13,12,10],[13,14,6],[2,3,14],[14,3,12],[14,10,4],[10,14,12],[14,4,5],[0,14,12],[9,14,1],[14,10,5],[14,10,8],[14,4,0],[7,0,14],[14,1,5],[12,9,5],[6,7,8],[7,4,12],[14,1,12],[8,14,2],[9,14,6],[3,8,6],[12,14,5],[14,7,1],[14,6,1],[1,14,2],[12,14,2],[1,14,9],[14,7,1],[12,8,2],[10,2,15],[8,11,14],[14,11,8]],[[8,3,0],[13,14,8],[12,2,14],[14,11,7],[14,0,2],[14,5,4],[14,8,12],[14,15,7],[14,7,2],[14,3,10],[14,2,4],[13,7,10],[1,14,12],[2,14,8],[11,9,14],[14,3,5],[12,10,14],[3,14,11],[9,14,0],[13,12,9],[8,14,12],[14,0,8],[14,11,6],[5,2,12],[14,13,5],[7,14,12],[6,9,10],[14,10,3],[1,15,5],[6,14,15],[13,9,14],[14,8,1],[14,4,15],[14,6,0],[2,14,5],[14,8,15],[15,14,6],[14,12,13],[14,4,1],[12,14,11],[14,6,2],[8,14,6],[15,14,8],[5,14,10],[5,14,3],[15,2,8],[14,9,4],[14,4,2],[14,8,1],[6,14,0],[13,9,10],[14,11,3],[10,5,14],[7,5,15],[9,4,6],[10,0,14],[14,2,0],[12,14,8],[12,14,2],[14,15,5],[14,5,11],[3,1,8],[12,14,15],[3,6,10],[8,14,10],[14,2,3],[14,8,6],[14,10,9],[4,14,8],[6,14,15],[14,5,4],[14,8,2],[14,1,9],[13,2,8],[14,5,6],[13,14,0],[14,15,11],[14,8,1],[12,14,3],[14,9,2],[10,3,12],[2,4,14],[0,14,10],[11,9,14],[14,0,1],[14,7,10],[15,14,0],[14,0,5],[10,14,6],[14,8,6],[8,14,13],[10,14,9],[14,1,11],[14,13,15],[3,14,12],[4,13,2],[11,14,15],[14,15,6],[6,14,0],[2,15,1],[9,13,12],[14,6,12],[0,14,4],[8,4,14],[14,13,9],[15,14,10],[3,7,14],[14,7,8],[10,5,13],[3,14,15],[8,9,13],[1,7,5],[7,9,14],[7,1,4],[3,2,1],[14,9,12],[12,15,14],[2,5,11],[14,15,4],[14,1,12],[14,5,1],[14,3,12],[14,8,12],[10,14,3],[14,7,6],[14,11,10],[14,9,7],[9,6,3],[6,3,14],[10,14,6],[2,0,14],[10,14,7],[14,10,1],[14,2,13],[8,14,10],[15,4,6],[14,0,13],[9,6,3],[14,6,12],[14,8,4],[14,8,10],[11,0,3],[14,10,12],[14,2,3],[14,10,15],[6,8,14],[10,12,14],[14,9,11],[15,4,14],[11,14,12],[14,10,0],[14,4,13],[14,13,3],[14,7,12],[14,7,12],[5,14,9],[6,14,12],[14,2,1],[14,7,10],[10,9,14],[0,11,14],[14,7,10],[14,3,2],[0,5,3],[5,14,15],[13,14,5],[6,13,5],[10,14,7],[14,13,7],[14,6,7],[2,11,9],[14,13,12],[14,12,15],[0,14,8],[6,14,12],[0,9,14],[10,4,12],[7,1,6],[13,5,0],[14,12,0],[14,9,4],[3,14,8],[14,13,10],[14,7,2],[1,14,2],[14,6,9],[6,14,11],[8,11,1],[10,4,14],[14,15,9],[14,8,10],[3,14,0],[15,14,13],[14,6,11],[10,12,14],[14,8,10],[14,9,11],[14,10,15],[14,4,15],[3,6,1],[6,11,14],[14,11,5],[14,9,13],[14,3,7],[14,11,7],[14,12,6],[3,14,4],[14,11,13],[3,7,14],[15,3,14],[14,9,11],[14,2,7],[14,3,11],[5,14,2],[14,1,9],[14,11,0],[6,5,14],[14,12,0],[7,0,10],[2,14,3],[15,14,8],[10,4,14],[14,1,2],[11,14,4],[14,5,4],[11,5,7],[4,2,14],[14,2,10],[14,10,5],[4,5,3],[14,4,7],[14,0,15],[0,3,14],[14,4,0],[1,14,6],[3,14,15],[12,14,13],[2,3,14],[14,11,6],[3,8,15],[14,10,12],[14,3,1],[0,14,3],[14,12,2],[14,13,12],[1,7,2],[14,9,5],[14,8,6],[14,11,6],[14,15,7],[14,13,10],[11,2,14],[14,12,8],[3,14,13],[5,8,4],[5,14,6]],[[8,9,14],[14,6,1],[14,5,8],[14,5,7],[14,6,5],[14,1,3],[14,6,8],[14,10,8],[14,5,9],[14,9,6],[11,0,13],[14,1,8],[4,14,11],[3,9,4],[14,1,5],[14,10,0],[7,9,14],[14,11,5],[6,2,8],[0,14,10],[1,12,0],[5,14,12],[8,11,2],[14,5,12],[1,4,14],[7,14,6],[14,1,3],[14,8,6],[2,14,0],[6,14,12],[13,6,14],[14,10,8],[14,7,11],[14,5,15],[3,14,9],[14,2,9],[14,4,0],[2,6,4],[14,5,12],[0,14,5],[14,7,11],[9,5,14],[14,1,12],[12,14,2],[0,14,6],[15,13,6],[6,14,4],[1,14,13],[14,11,12],[14,10,13],[14,7,4],[1,4,14],[7,5,14],[13,14,12],[14,1,9],[14,11,5],[14,8,1],[3,1,14],[14,2,5],[11,3,5],[14,4,11],[14,0,10],[5,14,15],[14,8,13],[3,12,13],[13,14,9],[14,4,12],[14,3,7],[14,0,8],[7,14,4],[8,7,2],[14,11,8],[2,7,14],[14,0,5],[14,10,12],[14,13,8],[14,15,3],[14,2,12],[13,12,14],[5,9,7],[14,8,12],[14,15,5],[9,15,13],[11,14,10],[14,11,7],[14,8,15],[11,8,14],[14,4,8],[7,0,3],[6,4,5],[2,13,14],[14,0,13],[14,4,10],[14,10,1],[14,13,1],[14,0,12],[14,11,15],[5,14,9],[12,14,8],[2,14,10],[8,5,13],[7,14,8],[14,12,15],[14,3,9],[14,8,12],[4,9,15],[10,7,14],[15,14,4],[14,15,5],[14,9,2],[14,2,0],[3,0,9],[3,14,13],[0,4,3],[14,5,10],[14,2,3],[10,14,1],[6,14,15],[14,0,1],[11,14,10],[14,7,4],[0,14,1],[14,4,9],[14,13,0],[14,5,4],[0,4,7],[13,2,14],[14,3,5],[9,15,14],[14,5,2],[9,14,15],[0,15,14],[3,14,7],[14,0,5],[4,2,5],[14,12,11],[5,14,7],[4,14,15],[1,14,7],[10,7,2],[14,13,15],[7,13,5],[0,6,15],[14,0,13],[14,10,9],[14,9,7],[2,3,5],[14,13,6],[13,4,5],[15,4,5],[14,6,1],[14,2,9],[14,7,12],[11,14,8],[14,0,5],[14,1,5],[14,11,4],[3,8,10],[10,12,11],[14,1,4],[3,14,6],[10,14,15],[14,13,3],[3,6,14],[14,7,15],[14,4,7],[14,7,10],[14,3,0],[5,14,8],[6,8,10],[14,11,0],[9,15,14],[5,4,14],[4,0,9],[1,14,9],[2,15,9],[3,14,2],[12,8,15],[14,7,13],[9,14,15],[14,2,6],[14,11,1],[14,5,10],[14,13,6],[14,0,11],[15,10,14],[14,1,6],[14,6,5],[10,0,8],[15,10,14],[14,7,4],[14,13,1],[6,14,0],[14,4,6],[6,14,2],[14,15,1],[14,12,0],[14,13,4],[11,14,12],[6,14,13],[4,11,14],[14,7,3],[14,10,0],[14,2,1],[14,5,12],[11,4,12],[2,14,5],[2,14,7],[6,4,14],[14,11,1],[10,14,0],[0,9,14],[7,13,6],[9,10,14],[4,8,14],[15,13,14],[14,1,4],[5,14,7],[14,0,13],[14,12,10],[14,10,0],[5,14,13],[0,13,14],[14,0,7],[14,15,2],[12,14,11],[7,12,13],[14,2,10],[7,8,12],[14,12,6],[14,15,4],[8,14,6],[14,5,1],[0,14,9],[13,14,6],[8,2,4],[15,14,13],[14,1,15],[13,5,14],[14,4,5],[12,14,6],[14,15,10],[2,11,7],[14,12,7],[4,5,14],[14,15,1],[14,5,13],[3,14,8],[0,14,13],[14,15,9],[11,14,2],[14,9,12],[2,6,13],[8,14,2],[14,8,11],[11,8,14]],[[14,8,13],[9,15,8],[14,15,3],[2,4,14],[14,3,11],[14,0,10],[10,12,11],[0,14,6],[14,0,10],[14,0,7],[14,9,2],[8,14,11],[14,11,9],[14,2,4],[11,15,14],[8,14,0],[5,14,15],[6,11,14],[14,15,13],[7,14,1],[3,2,14],[0,2,9],[13,10,3],[12,3,0],[14,11,13],[14,0,3],[5,9,12],[14,4,0],[14,8,3],[14,1,4],[14,5,4],[2,13,14],[8,14,11],[10,5,14],[14,10,12],[13,2,3],[1,14,5],[14,1,13],[7,14,11],[7,14,13],[14,1,15],[8,6,12],[11,14,5],[14,7,15],[14,12,5],[14,11,2],[14,1,15],[14,10,13],[9,12,7],[8,14,13],[14,11,8],[4,14,0],[14,7,9],[14,0,2],[14,11,0],[14,4,0],[14,9,5],[7,12,0],[14,0,5],[0,14,6],[4,5,11],[15,14,8],[14,8,13],[14,5,2],[14,5,9],[14,13,5],[14,6,5],[0,14,2],[2,9,7],[15,3,9],[6,3,8],[14,8,0],[6,14,12],[13,14,15],[14,11,6],[11,3,7],[1,14,0],[14,5,9],[0,4,11],[14,5,13],[4,14,15],[14,6,12],[10,14,9],[14,12,11],[15,12,14],[14,11,4],[14,15,3],[7,14,1],[6,4,14],[14,11,12],[10,14,15],[12,5,11],[13,14,0],[14,6,15],[13,14,3],[2,6,4],[13,5,14],[14,8,15],[15,10,8],[11,14,9],[10,0,12],[14,11,9],[8,14,10],[4,7,14],[3,8,14],[4,13,3],[14,8,3],[14,10,0],[12,14,6],[14,6,11],[1,12,7],[12,14,1],[14,2,3],[14,5,3],[14,3,9],[12,4,14],[8,9,11],[14,9,1],[14,5,2],[6,9,14],[8,7,14],[10,0,3],[13,15,14],[7,13,14],[14,13,3],[13,8,11],[10,7,5],[8,14,4],[2,14,1],[5,0,3],[7,14,0],[14,11,5],[9,14,3],[0,14,2],[14,15,5],[5,9,14],[14,3,13],[14,10,6],[15,14,12],[1,14,15],[14,6,9],[14,12,9],[14,10,8],[7,1,14],[14,13,7],[10,14,9],[14,10,0],[2,14,7],[6,8,14],[14,2,4],[6,0,11],[15,9,14],[7,14,15],[12,14,8],[14,10,8],[14,12,2],[2,12,14],[9,14,4],[13,12,14],[14,4,0],[14,12,3],[5,11,14],[6,14,15],[9,14,7],[2,14,13],[15,6,0],[9,13,4],[3,9,15],[13,14,15],[12,4,14],[5,4,6],[12,8,14],[14,11,2],[8,0,14],[8,2,14],[1,3,6],[5,14,12],[2,0,14],[3,7,14],[7,0,9],[12,14,1],[9,14,10],[6,14,5],[14,13,9],[14,6,4],[7,14,15],[14,9,7],[2,14,3],[14,10,8],[14,9,2],[5,10,4],[4,14,3],[14,12,9],[14,6,7],[6,14,2],[9,14,12],[14,11,2],[14,4,3],[2,14,5],[10,9,1],[14,12,1],[2,14,12],[9,14,11],[14,0,13],[14,5,7],[14,11,15],[14,3,10],[14,13,15],[14,12,5],[14,5,11],[14,4,13],[14,13,9],[14,9,6],[13,15,14],[14,7,9],[14,10,8],[14,0,6],[2,14,15],[11,4,10],[14,3,7],[9,4,14],[14,3,0],[14,7,5],[14,13,2],[9,14,7],[14,2,11],[11,14,1],[14,1,10],[13,14,4],[13,11,14],[7,14,8],[12,8,5],[10,14,6],[9,14,6],[14,2,15],[14,5,0],[7,14,11],[11,14,4],[14,0,10],[14,8,11],[14,13,5],[14,11,7],[12,15,2],[12,10,14],[6,14,13],[15,14,8],[4,14,6],[13,11,14],[14,12,6],[14,4,9],[10,13,14],[1,14,8],[2,15,14],[11,14,12],[2,14,11],[14,3,4]],[[7,8,1],[14,5,6],[10,2,4],[2,14,6],[14,10,7],[7,14,12],[11,14,6],[11,15,6],[13,14,7],[11,15,14],[14,15,13],[4,14,2],[14,11,12],[14,15,13],[13,14,6],[14,8,3],[9,14,15],[13,14,10],[8,14,10],[14,12,6],[14,5,6],[14,1,8],[4,3,2],[14,13,6],[14,9,8],[15,14,8],[14,11,12],[14,2,11],[15,12,14],[12,14,7],[11,14,3],[4,5,12],[15,14,6],[8,14,5],[5,3,0],[0,14,7],[3,9,6],[14,10,11],[14,11,5],[4,15,14],[15,13,14],[14,12,11],[14,6,5],[12,14,0],[14,8,0],[6,4,0],[14,10,0],[14,12,3],[10,9,12],[1,14,2],[12,14,4],[9,8,14],[12,7,14],[4,14,13],[8,14,1],[8,12,14],[3,15,5],[4,14,13],[10,2,12],[10,0,4],[10,14,11],[14,2,7],[8,3,14],[10,14,6],[10,12,14],[2,1,14],[8,13,10],[14,5,4],[15,14,12],[14,9,12],[6,14,8],[14,13,7],[12,14,11],[14,3,2],[0,14,10],[0,10,11],[4,14,13],[14,9,6],[14,12,5],[14,5,2],[14,3,13],[14,9,13],[10,14,11],[11,2,14],[9,7,14],[14,9,12],[5,0,11],[15,14,9],[14,10,3],[13,14,15],[3,14,11],[3,4,14],[12,15,14],[14,5,7],[14,0,15],[12,14,10],[9,14,8],[14,0,2],[14,2,5],[14,2,6],[9,11,14],[11,6,2],[15,4,2],[14,1,4],[14,12,15],[7,0,15],[14,5,8],[14,9,10],[14,15,13],[0,14,6],[14,15,1],[4,14,8],[15,7,14],[14,11,1],[14,3,2],[2,14,0],[14,6,9],[14,3,11],[14,0,7],[15,14,11],[7,14,6],[3,14,7],[14,6,13],[14,1,12],[6,0,14],[6,14,0],[14,3,5],[6,14,11],[4,14,3],[1,14,4],[14,9,13],[0,14,6],[14,11,15],[2,5,14],[14,10,5],[4,8,6],[14,7,13],[14,10,13],[14,2,0],[14,13,12],[14,12,4],[2,15,13],[14,6,2],[8,14,6],[10,14,6],[9,14,2],[2,14,6],[14,5,12],[14,10,12],[10,9,14],[4,14,12],[6,14,8],[4,14,12],[14,7,10],[0,12,14],[13,14,2],[14,11,4],[14,8,7],[11,14,3],[14,6,9],[10,12,14],[12,8,13],[6,14,9],[14,7,8],[2,14,13],[15,3,7],[14,4,3],[11,14,7],[11,6,7],[14,8,12],[0,9,14],[14,15,7],[15,6,4],[5,14,13],[13,14,1],[14,9,5],[14,0,5],[14,13,4],[6,14,4],[14,4,2],[14,7,12],[14,15,1],[14,3,10],[3,14,7],[9,14,1],[14,9,13],[14,5,0],[0,10,14],[2,14,15],[8,14,4],[14,6,13],[14,13,0],[14,11,3],[14,11,5],[14,10,5],[9,8,15],[10,14,4],[3,14,13],[14,15,10],[14,6,12],[14,6,10],[0,8,14],[12,10,5],[14,3,15],[0,4,5],[14,0,13],[3,8,14],[5,1,4],[14,4,9],[14,2,9],[14,9,0],[14,7,0],[0,15,14],[3,5,14],[4,3,14],[14,0,7],[8,14,1],[7,2,14],[11,1,14],[14,7,15],[14,13,9],[5,14,8],[15,14,1],[14,15,7],[14,2,4],[2,10,0],[10,1,14],[3,15,1],[14,3,12],[13,7,9],[14,0,3],[14,4,5],[0,8,13],[14,10,1],[14,13,6],[14,13,1],[12,14,1],[3,10,14],[7,15,14],[14,13,7],[14,4,12],[14,1,2],[14,5,7],[1,13,14],[13,11,14],[1,11,5],[14,5,10],[6,12,13],[14,4,11],[14,8,12],[9,2,13],[14,8,13],[14,8,3],[2,14,5],[1,14,4],[14,6,12]],[[12,14,0],[14,9,5],[2,11,5],[13,2,9],[14,5,12],[14,8,12],[14,6,15],[15,5,8],[14,15,7],[14,8,3],[14,10,6],[15,6,2],[3,4,12],[14,5,10],[14,1,0],[14,3,9],[14,12,3],[6,12,14],[4,13,8],[10,9,6],[14,4,12],[14,12,13],[10,14,0],[1,12,14],[14,6,15],[11,3,13],[8,13,6],[4,9,14],[14,3,10],[14,13,3],[9,15,11],[12,3,14],[14,1,2],[14,8,3],[4,6,3],[12,6,14],[12,1,2],[14,3,2],[2,4,1],[14,5,9],[7,14,12],[14,10,1],[14,8,15],[12,14,8],[14,1,0],[14,1,12],[8,14,6],[12,14,1],[14,1,0],[10,14,13],[14,12,7],[15,14,0],[5,2,14],[14,11,2],[1,7,15],[7,14,0],[6,14,1],[5,14,2],[3,14,9],[14,6,10],[7,14,11],[14,13,7],[2,7,14],[2,14,10],[7,14,4],[14,11,4],[1,14,2],[5,8,14],[4,15,14],[14,0,1],[14,2,7],[7,4,1],[8,0,3],[14,5,1],[14,2,6],[14,7,8],[14,9,15],[14,13,6],[9,8,14],[3,14,0],[14,10,2],[14,1,10],[2,0,14],[12,0,7],[0,14,11],[5,3,14],[15,14,2],[0,14,13],[5,14,1],[6,14,11],[7,3,14],[10,1,14],[5,14,11],[14,3,11],[14,10,4],[14,10,11],[14,10,12],[10,15,8],[14,6,4],[12,14,5],[14,15,2],[10,12,9],[10,14,8],[5,2,9],[14,10,1],[9,2,14],[14,4,5],[14,0,12],[13,3,10],[14,2,5],[14,4,2],[0,14,2],[11,5,15],[14,10,8],[9,14,15],[5,0,8],[14,1,8],[14,13,0],[0,14,9],[7,8,1],[4,11,7],[14,15,9],[3,14,10],[4,11,10],[10,1,6],[0,5,1],[14,10,7],[14,15,12],[5,14,8],[14,4,2],[3,7,0],[14,1,15],[10,2,15],[5,3,14],[5,14,13],[9,14,2],[14,10,11],[14,2,10],[11,8,1],[9,10,1],[9,14,8],[14,15,7],[8,9,1],[14,13,7],[14,13,2],[10,14,3],[8,3,4],[5,11,12],[14,6,10],[7,14,9],[14,6,4],[3,7,14],[14,3,13],[5,14,7],[13,7,14],[10,6,8],[0,5,14],[1,8,14],[1,14,6],[11,8,13],[14,13,4],[5,0,1],[10,0,14],[14,11,4],[14,10,8],[14,0,2],[5,10,8],[14,7,9],[14,3,5],[10,11,14],[12,14,6],[14,11,5],[4,14,9],[14,0,9],[12,14,4],[9,14,0],[14,3,8],[14,1,5],[15,14,11],[14,15,6],[14,1,9],[14,7,6],[14,8,5],[13,12,6],[13,7,11],[8,14,7],[6,14,5],[14,13,6],[14,5,4],[14,4,0],[14,10,8],[12,14,9],[13,14,6],[14,3,8],[14,8,7],[14,2,6],[8,5,7],[14,2,0],[9,4,14],[14,13,3],[14,11,6],[14,8,6],[14,5,3],[8,14,1],[2,9,14],[4,14,12],[7,14,12],[14,5,7],[14,6,9],[14,5,6],[12,14,1],[14,9,5],[6,14,9],[13,14,7],[10,14,13],[1,14,13],[4,10,9],[10,0,4],[14,15,9],[6,2,13],[14,0,12],[3,14,13],[9,15,1],[14,15,13],[14,1,15],[14,12,3],[9,14,0],[14,0,5],[14,8,1],[1,8,15],[10,14,1],[12,8,3],[7,13,14],[14,7,3],[14,4,2],[5,1,11],[4,14,8],[14,1,12],[10,14,6],[14,10,11],[14,0,4],[14,11,9],[3,4,14],[14,0,9],[7,14,10],[14,11,9],[14,8,6],[5,4,11],[14,9,8],[2,4,1],[8,9,15],[9,14,11],[14,9,5],[13,14,8],[6,14,11],[10,14,4]],[[5,14,0],[5,14,12],[4,9,12],[14,2,11],[14,3,4],[14,5,4],[3,11,2],[14,12,2],[8,14,12],[15,14,4],[12,4,14],[8,9,10],[13,14,5],[7,3,14],[8,7,12],[8,14,3],[14,2,5],[14,15,9],[14,13,7],[2,14,9],[0,14,3],[14,13,15],[14,12,3],[14,9,5],[7,14,6],[6,9,14],[10,9,14],[3,5,12],[1,14,12],[14,13,11],[10,14,7],[14,11,1],[9,1,7],[14,7,15],[13,14,3],[11,14,15],[14,2,7],[11,14,6],[14,12,10],[3,14,11],[1,10,14],[14,8,11],[0,13,6],[14,2,3],[14,8,10],[14,0,7],[14,12,15],[15,14,6],[14,15,5],[14,3,9],[6,14,5],[2,5,14],[14,0,10],[12,14,6],[14,10,6],[14,2,4],[4,14,15],[14,0,15],[14,0,6],[0,11,14],[5,14,2],[14,13,7],[7,14,13],[14,3,15],[8,12,2],[14,3,5],[8,3,14],[11,14,7],[3,14,6],[13,2,9],[8,14,6],[14,1,8],[8,9,13],[14,7,2],[6,14,11],[15,0,12],[14,15,5],[14,10,2],[15,1,14],[11,0,14],[0,14,12],[14,4,7],[14,0,3],[14,3,9],[2,14,0],[1,14,12],[12,9,14],[3,9,7],[15,14,9],[14,3,8],[14,9,5],[11,6,14],[14,1,15],[3,14,6],[15,14,10],[14,9,13],[14,5,9],[14,10,9],[14,13,5],[2,14,1],[14,15,7],[14,8,11],[14,0,1],[14,5,12],[14,8,6],[15,2,8],[0,14,15],[14,4,13],[14,5,15],[1,0,6],[14,5,7],[0,1,14],[14,7,11],[4,5,11],[6,2,15],[13,14,7],[2,13,14],[1,14,7],[14,12,3],[2,7,15],[5,0,1],[14,7,4],[14,0,3],[14,3,15],[14,8,9],[9,4,7],[11,14,12],[8,14,3],[2,11,13],[14,4,7],[6,12,7],[10,14,12],[9,14,12],[5,14,12],[14,5,8],[13,14,6],[1,11,14],[14,4,5],[15,1,14],[5,10,6],[5,14,0],[14,10,6],[14,13,0],[14,15,8],[14,15,6],[12,15,2],[14,7,8],[11,12,5],[14,2,10],[14,3,2],[14,3,2],[14,12,10],[7,11,14],[14,8,7],[14,10,0],[14,9,0],[14,1,3],[14,2,3],[14,0,5],[2,14,11],[0,1,5],[14,0,13],[11,12,13],[14,11,3],[14,15,12],[14,10,6],[9,12,14],[5,14,11],[7,4,14],[14,13,0],[6,14,9],[14,13,3],[6,14,5],[14,10,15],[14,0,4],[2,4,12],[4,5,14],[15,11,14],[14,5,15],[14,9,15],[1,7,4],[7,14,6],[9,1,3],[4,0,11],[8,10,7],[14,13,4],[2,14,0],[14,10,3],[13,2,4],[14,6,8],[10,14,5],[14,5,13],[14,5,11],[14,15,6],[14,11,7],[13,11,1],[14,13,11],[4,10,14],[14,0,10],[14,3,8],[3,11,5],[14,0,7],[11,14,8],[14,7,4],[0,5,9],[14,3,9],[7,12,0],[14,2,11],[12,13,8],[9,14,13],[12,14,0],[14,6,0],[3,8,15],[14,3,4],[14,15,2],[13,14,2],[10,14,13],[11,8,6],[5,6,3],[6,14,13],[14,6,9],[15,12,14],[13,14,15],[1,15,14],[14,1,3],[14,10,9],[15,3,14],[4,13,6],[14,4,3],[14,10,4],[9,4,14],[15,14,6],[12,3,14],[2,14,10],[14,13,0],[14,12,0],[14,4,12],[14,1,3],[14,12,6],[3,13,9],[14,13,12],[3,4,14],[14,2,1],[14,12,4],[14,15,6],[14,8,7],[14,15,0],[14,1,9],[14,13,15],[8,14,9],[14,8,13],[13,7,14],[11,14,8],[14,0,13],[2,14,11],[4,14,10]],[[14,6,10],[14,2,13],[6,2,4],[14,11,3],[9,13,15],[13,6,14],[1,3,14],[14,7,4],[14,5,8],[14,9,4],[7,11,6],[6,14,13],[14,10,7],[11,1,4],[14,7,8],[9,15,14],[12,14,2],[14,1,10],[13,14,4],[14,12,2],[0,5,3],[14,10,9],[6,14,9],[14,11,13],[5,4,7],[14,2,1],[10,14,8],[14,6,0],[14,15,6],[14,9,7],[14,11,9],[1,6,11],[14,12,8],[14,8,9],[14,15,10],[14,2,1],[14,1,0],[14,12,3],[9,0,14],[9,14,0],[14,0,4],[2,5,14],[5,14,3],[12,14,5],[14,7,2],[4,15,14],[1,14,7],[2,10,14],[14,9,1],[14,12,2],[2,9,7],[14,4,3],[2,13,14],[14,4,3],[4,14,9],[6,5,10],[3,5,14],[3,14,8],[13,14,12],[10,8,14],[14,10,13],[14,6,0],[14,15,6],[14,12,6],[7,12,11],[14,12,1],[14,12,4],[14,8,7],[14,2,3],[1,14,4],[5,1,14],[15,11,2],[14,8,11],[11,12,14],[14,3,15],[7,14,10],[2,8,3],[13,9,5],[14,9,12],[14,13,2],[14,9,15],[6,4,13],[14,3,13],[12,14,4],[3,11,14],[14,8,0],[8,14,11],[14,0,10],[8,14,7],[14,10,1],[4,11,14],[6,5,14],[12,13,6],[14,8,2],[14,15,13],[14,11,9],[14,2,6],[2,5,4],[3,14,11],[0,2,14],[8,14,3],[1,10,7],[14,2,12],[11,3,15],[12,13,0],[3,2,14],[9,14,15],[11,0,14],[7,14,4],[14,5,1],[14,15,8],[8,14,4],[14,8,10],[0,14,5],[14,3,2],[10,0,3],[14,2,9],[14,6,13],[5,9,14],[15,6,1],[3,14,1],[9,14,13],[6,11,0],[3,14,0],[14,4,1],[11,14,1],[14,1,2],[14,1,7],[14,12,4],[14,10,1],[6,9,2],[13,14,2],[0,11,14],[14,7,13],[3,14,6],[11,14,10],[14,11,12],[14,8,0],[15,0,14],[11,5,14],[7,14,5],[13,2,14],[6,14,4],[14,3,8],[11,5,14],[10,12,14],[4,14,11],[2,5,12],[8,14,10],[14,3,13],[14,12,7],[3,14,1],[14,13,12],[0,14,12],[0,14,11],[3,14,9],[14,7,9],[10,14,8],[5,15,7],[14,3,6],[0,14,11],[9,14,6],[3,11,14],[14,5,4],[14,12,15],[9,0,12],[14,8,7],[14,10,7],[14,10,13],[14,11,2],[10,14,5],[2,14,1],[13,14,7],[8,12,11],[14,13,0],[10,14,12],[11,14,10],[11,14,9],[3,14,5],[1,14,4],[10,14,15],[14,2,7],[4,12,6],[11,3,14],[15,5,9],[14,13,7],[14,12,13],[14,0,4],[14,4,13],[14,11,5],[14,1,7],[11,14,6],[4,1,14],[12,14,0],[4,9,14],[4,14,11],[14,15,9],[14,8,0],[4,10,14],[14,3,5],[14,0,8],[7,14,9],[14,9,3],[14,1,9],[5,8,11],[1,14,4],[14,1,9],[12,14,15],[3,14,12],[14,9,11],[14,6,4],[7,14,8],[5,14,15],[14,5,4],[4,11,14],[6,14,0],[15,5,12],[12,5,14],[14,1,7],[14,0,9],[11,7,14],[14,7,15],[14,1,6],[14,13,5],[14,3,12],[14,15,11],[12,0,9],[11,7,6],[14,10,12],[14,6,3],[14,0,8],[6,14,15],[10,8,11],[13,2,0],[14,0,1],[14,8,2],[7,14,3],[11,9,15],[12,8,9],[5,2,14],[1,14,5],[1,9,14],[11,4,15],[1,12,4],[6,14,3],[14,3,5],[14,15,13],[14,13,7],[14,8,1],[12,14,2],[5,1,14],[0,14,5],[4,14,9],[5,14,10],[11,14,7],[14,11,6]]]
CAP = 745
YW = 745
def setup_inputs(rng):
    return {"x": rng.standard_normal((N, 128, T), dtype=np.float32).astype(ml_dtypes.bfloat16)}
def reference(x):
    y = np.full((N, 128, YW), np.nan, x.dtype)
    fill = [0] * N
    for r in range(N):
        for t in range(T):
            for e in ROUTE[r][t]:
                if fill[e] < CAP:
                    y[e][:, fill[e]] = x[r][:, t]
                fill[e] += 1
    return {"y": y}

import numpy as np
import comms_topo

NSLOT = 8
SCRATCH = {
    "xs": ("sbuf", [128, 256], "bfloat16"),
    "pack": ("sbuf", [128, 768], "bfloat16"),
    "land": ("sbuf", [128, 745], "bfloat16"),
}
SEMAPHORES = (["loaded", "xin", "sent", "arrived", "stored"]
              + ["pg%d" % j for j in range(NSLOT)] + ["ph%d" % j for j in range(NSLOT)])

PLANS = {}


def make_plan(tables, cores):
    topo = comms_topo
    route, cap = tables["ROUTE"], tables["CAP"]
    n, nt = len(route), len(route[0])
    fill = [0] * n
    kept = [[[] for e in range(n)] for r in range(n)]
    base = [[0] * n for r in range(n)]
    for r in range(n):
        for e in range(n):
            base[r][e] = min(fill[e], cap)
        for t, es in enumerate(route[r]):
            for e in es:
                if fill[e] < cap:
                    kept[r][e].append(t)
                fill[e] += 1
    count = [min(f, cap) for f in fill]
    chip = [topo.chip(c) for c in cores]
    rank_on = {chip[r]: r for r in range(n)}

    def experts(r, far):
        return [e for e in range(n) if kept[r][e] and bool((chip[e] ^ chip[r]) & 1) == far]

    def prefixes(r, far):
        pa, ps, pr, cut = (np.zeros(nt + 1, dtype=np.int64) for i in range(4))
        for e in experts(r, far):
            s = set(kept[r][e])
            for t in s:
                if e != r:
                    pa[t + 1] += 1
                    if not topo.mates(chip[r], chip[e]):
                        ps[t + 1] += 1
                if t - 1 in s:
                    cut[t] += 1
                else:
                    pr[t + 1] += 1
        return np.cumsum(pa), np.cumsum(ps), np.cumsum(pr), cut

    pre = {(r, far): prefixes(r, far) for r in range(n) for far in (False, True)}

    def through(r):
        m = rank_on.get(chip[r] ^ 1)
        return int(pre[(r, False)][1][nt]), (int(pre[(m, True)][1][nt]) if m is not None else 0)

    t_sw = max((sum(through(r)) + 1) // 2 for r in range(n))
    t_mate = max((int(pre[(r, True)][0][nt]) + 1) // 2 for r in range(n))

    def group(r, far):
        first = chip[r] * topo.CORES_PER_CHIP
        by_die = {0: [], 1: []}
        for c in range(first, first + topo.CORES_PER_CHIP):
            if topo.may_write(c, c ^ topo.CORES_PER_CHIP) == far:
                by_die[topo.die(c)].append(c)
        return by_die

    def choose(r, far, lim_sw, lim_mate):
        pa, ps, pr, cut = pre[(r, far)]
        by_die = group(r, far)
        home = topo.die(cores[r]) if cores[r] in by_die[topo.die(cores[r])] else None
        win = np.arange(-22, 23)
        mid = [int(np.searchsorted(pr, pr[nt] * k / 4.0)) for k in (1, 2, 3)]
        b1, b2, b3 = np.meshgrid(*[np.clip(m + win, 1, nt - 1) for m in mid], indexing="ij")
        ok = (b1 < b2) & (b2 < b3)
        bs = [np.zeros_like(b1), b1, b2, b3, np.full_like(b1, nt)]
        sw = [ps[bs[i + 1]] - ps[bs[i]] for i in range(4)]
        al = [pa[bs[i + 1]] - pa[bs[i]] for i in range(4)]
        nd = [pr[bs[i + 1]] - pr[bs[i]] + cut[bs[i]] for i in range(4)]
        best = None
        for dies in ((0, 1, 1, 0), (1, 0, 0, 1), (0, 1, 0, 1), (1, 0, 1, 0)):
            seg = {d: [i for i in range(4) if dies[i] == d] for d in (0, 1)}
            over, busy = 0, 0
            for d in (0, 1):
                i, j = seg[d]
                over = over + np.maximum(0, sw[i] + sw[j] - lim_sw[d]) + np.maximum(0, al[i] + al[j] - lim_mate[d])
                hi, lo = np.maximum(nd[i], nd[j]), np.minimum(nd[i], nd[j])
                busy = np.maximum(busy, np.maximum(hi, lo + 2) if d == home else hi)
            i, j = seg[0]
            skew = np.abs(2 * (sw[i] + sw[j]) - ps[nt]) + np.abs(2 * (al[i] + al[j]) - pa[nt])
            cost = np.where(ok, 10000 * over + 6 * busy + skew, 10 ** 9)
            k = int(np.argmin(cost))
            if best is None or cost.flat[k] < best[0]:
                best = (int(cost.flat[k]), dies, [int(b.flat[k]) for b in bs], [int(x.flat[k]) for x in nd],
                        [int(x.flat[k]) for x in sw])
        dies, cuts, nds, sws = best[1:]
        out, load = [], [0, 0]
        for d in (0, 1):
            segs = [i for i in range(4) if dies[i] == d]
            pair = list(by_die[d])
            if d == home:
                segs.sort(key=lambda i: nds[i])
                pair.sort(key=lambda c: c != cores[r])
            for i, c in zip(segs, pair):
                out.append((c, cuts[i], cuts[i + 1]))
                load[d] += sws[i]
        return out, load

    jobs = {}
    for r in range(n):
        a, b = through(r)
        room = max(0, t_sw - (a + 1) // 2 - (b + 1) // 2) // 2
        lim = (a + 1) // 2 + room
        got, load = choose(r, False, (lim, lim), (10 ** 6, 10 ** 6))
        for c, lo, hi in got:
            jobs[c] = (r, lo, hi, experts(r, False))
        m = rank_on.get(chip[r] ^ 1)
        if m is not None:
            got, load = choose(m, True, (t_sw - load[0], t_sw - load[1]), (t_mate, t_mate))
            for c, lo, hi in got:
                jobs[c] = (m, lo, hi, experts(m, True))
    return kept, base, count, jobs


def blocks_of(plan, core):
    kept, base, count, jobs = plan
    if core not in jobs:
        return []
    r, lo, hi, experts = jobs[core]
    out = []
    for e in experts:
        before = sum(1 for t in kept[r][e] if t < lo)
        runs = []
        for t in kept[r][e]:
            if lo <= t < hi:
                if runs and runs[-1][0] + runs[-1][1] == t:
                    runs[-1][1] += 1
                else:
                    runs.append([t, 1])
        if runs:
            out.append((e, runs, sum(run[1] for run in runs), base[r][e] + before))
    return out


def engines(mask):
    return bin(mask).count("1")


def rank_program(g, core, T, topo):
    cores = list(T.cores)
    if "p" not in PLANS:
        PLANS["p"] = make_plan(T.tables, cores)
    plan = PLANS["p"]
    kept, base, count, jobs = plan
    if core not in jobs:
        return
    rank = T.rank_of(core)
    r = jobs[core][0]
    sent = 0

    def write(dst, dst_ap, src_ap, sem):
        rid, pid = topo.addr(dst)[0:2]
        m = topo.mask(core, dst)
        g.remote_dma(dst_ap, src_ap, sem, T.sem.sent, pid, rid, m)
        return engines(m)

    queues = [g.sync, g.scalar, g]
    if rank is not None:
        g.sync.dma_start(T.xs[:], T.x[:]).then_inc(T.sem.loaded, 16)
        for q in queues:
            q.wait_ge(T.sem.loaded, 16)
        for c in sorted(jobs):
            if c != core and jobs[c][0] == rank:
                a, b = jobs[c][1], jobs[c][2]
                sent += write(c, T.xs[:, a:b], T.xs[:, a:b], T.sem.xin)
    else:
        for q in queues:
            q.wait_ge(T.sem.xin, engines(topo.mask(cores[r], core)))

    blocks = blocks_of(plan, core)
    waits, col, i = [], 0, 0
    for j, (e, runs, k, pos) in enumerate(blocks):
        here = cores[e] == core
        buf, o = (T.land, pos) if here else (T.pack, col)
        cnt = [0, 0]
        for t, w in runs:
            q = queues[i % 3]
            soft = q is g
            q.dma_start(buf[:, o:o + w], T.xs[:, t:t + w]).then_inc(T.sem[("pg%d" if soft else "ph%d") % j], 16)
            cnt[1 if soft else 0] += 16
            o += w
            i += 1
        waits.append(cnt)
        if not here:
            col += k

    col = 0
    for j, (e, runs, k, pos) in enumerate(blocks):
        if waits[j][0]:
            g.wait_ge(T.sem["ph%d" % j], waits[j][0])
        if waits[j][1]:
            g.wait_ge(T.sem["pg%d" % j], waits[j][1])
        if cores[e] != core:
            sent += write(cores[e], T.land[:, pos:pos + k], T.pack[:, col:col + k], T.sem.arrived)
            col += k
    g.wait_ge(T.sem.sent, sent)

    if rank is not None:
        due = 0
        for c in sorted(jobs):
            if c != core:
                due += sum(engines(topo.mask(c, core)) for b in blocks_of(plan, c) if b[0] == rank)
        g.wait_ge(T.sem.arrived, due)
        g.dma_start(T.y[:, 0:count[rank]], T.land[:, 0:count[rank]]).then_inc(T.sem.stored, 16)
        g.wait_ge(T.sem.stored, 16)
